import numpy as np
import ml_dtypes


def mxq(x, axis, fmt="e4m3"):
    dtype, down = {"e4m3": (ml_dtypes.float8_e4m3fn, 7), "e5m2": (ml_dtypes.float8_e5m2, 14)}[fmt]
    v = np.moveaxis(np.asarray(x, np.float32).astype(ml_dtypes.bfloat16).astype(np.float64), axis, -1)
    blocks = v.reshape(v.shape[:-1] + (-1, 32))
    amax = np.abs(blocks).max(-1, keepdims=True)
    byte = np.maximum(np.where(amax > 0, np.frexp(amax)[1] - 1 + 127, 0) - down, 1)
    scale = np.exp2(byte - 127.0)
    codes = (blocks / scale).astype(np.float32).astype(dtype).astype(np.float64)
    return np.moveaxis((codes * scale).reshape(v.shape), -1, axis)


WIDE = False


def mx_kscale(k):
    if not WIDE:
        return np.ones(k)
    levels = np.array([10, -10, 5, -5, 0])
    if k % 512:
        return np.exp2(np.random.permutation(np.resize(levels, k // 32))).repeat(32)
    a = np.empty((k // 512, 16))
    for p in range(k // 512):
        a[p, :8] = np.random.permutation(np.resize(levels, 8))
        for g in range(8):
            far = levels[np.abs(levels - a[p, g]) >= 10]
            a[p, g + 8] = far[np.random.randint(len(far))]
    return np.exp2(a.ravel()).repeat(32)


def f64(x):
    return np.asarray(x).astype(np.float64)


def striped(idx):
    return np.tile(idx.reshape(-1, 16).T, (8, 1)).astype(np.uint16)


def unstriped(offs):
    return offs[:16].T.reshape(-1).astype(np.int64)


def striped8(idx):
    return np.concatenate([x.reshape(-1, 16).T for x in idx]).astype(np.uint16)


def runs(offs, k):
    lists = np.stack([offs[16 * r : 16 * r + 16].T.reshape(-1) for r in range(8)]).astype(np.int64)
    return lists[np.arange(k) % 512 // 64]


def pack_weight(w):
    k, n = w.shape
    w = f64(np.asarray(w, np.float32).astype(ml_dtypes.bfloat16)).reshape(k // 32, 32, n)
    amax = np.abs(w).max(1)
    byte = np.clip(np.where(amax > 0, np.frexp(amax)[1] - 1 + 127 - 7, 1), 1, 254)
    scaled = (w * np.exp2(127.0 - byte)[:, None, :]).reshape(k, n).astype(np.float32)
    words = np.ascontiguousarray(scaled.reshape(k // 512, 128, 4, n).transpose(0, 1, 3, 2)).astype(ml_dtypes.float8_e4m3fn).view(np.uint8)
    return words, np.ascontiguousarray(byte.astype(np.uint8).reshape(k // 512, 16, n))


def unpack_weight(words, scales):
    g, p, n, _ = words.shape
    vals = np.ascontiguousarray(words).view(ml_dtypes.float8_e4m3fn).astype(np.float64) * np.repeat(np.exp2(scales.astype(np.float64) - 127.0), 8, axis=1)[..., None]
    return vals.transpose(0, 1, 3, 2).reshape(g * 512, n)


E2M1 = np.array([0.0, 0.5, 1.0, 1.5, 2.0, 3.0, 4.0, 6.0, -0.0, -0.5, -1.0, -1.5, -2.0, -3.0, -4.0, -6.0])


def pack_fp4(w):
    k, n = w.shape
    w = f64(np.asarray(w, np.float32).astype(ml_dtypes.bfloat16)).reshape(k // 32, 32, n)
    amax = np.abs(w).max(1)
    mant, ex = np.frexp(amax / 6.0)
    byte = np.clip(np.where(amax > 0, np.where(mant > 0.5, ex, ex - 1) + 127, 1), 1, 254)
    scaled = (w * np.exp2(127.0 - byte)[:, None, :]).reshape(k, n).astype(np.float32)
    c = np.ascontiguousarray(scaled.reshape(k // 512, 128, 4, n).transpose(0, 1, 3, 2)).astype(ml_dtypes.float4_e2m1fn).view(np.uint8) & 0xF
    words = (c[..., 0::2] | (c[..., 1::2] << 4)).reshape(k // 512, 128, 2 * n)
    return np.ascontiguousarray(words), np.ascontiguousarray(byte.astype(np.uint8).reshape(k // 512, 16, n))


def unpack_fp4(words, scales):
    g, _, n = scales.shape
    words = np.ascontiguousarray(words).reshape(g, 128, n, 2)
    nib = np.empty((g, 128, n, 4), np.uint8)
    nib[..., 0::2] = words & 0xF
    nib[..., 1::2] = words >> 4
    vals = E2M1[nib] * np.repeat(np.exp2(scales.astype(np.float64) - 127.0), 8, axis=1)[..., None]
    return vals.transpose(0, 1, 3, 2).reshape(g * 512, n)


def sigmoid(v):
    return 1.0 / (1.0 + np.exp(-np.maximum(v, -700.0)))

def planes(y):
    n, m = y.shape
    v = y.astype(np.float32).astype(ml_dtypes.bfloat16).astype(np.float64).reshape(n // 32, 32, m)
    top = np.abs(v).max(1)
    byte = np.clip(np.where(top > 0, np.frexp(top)[1] - 1 + 127 - 7, 1), 1, 254)
    codes = (v * np.exp2(127.0 - byte)[:, None, :]).reshape(n, m).astype(np.float32).astype(ml_dtypes.float8_e4m3fn).view(np.uint8)
    words = codes.reshape(n // 512, 128, 4, m).transpose(0, 1, 3, 2)
    return np.ascontiguousarray(words), np.ascontiguousarray(byte.astype(np.uint8).reshape(n // 512, 16, m))


K, T, S, N, H = 512, 2048, 512, 512, 512


def setup_inputs():
    n = np.random.standard_normal
    s = mx_kscale(K)[:, None]
    u = mx_kscale(H)
    packed_xT = pack_weight(n((K, T)) * s)
    packed_w1 = pack_fp4(n((K, H)) / np.sqrt(K) / s)
    packed_w2 = pack_fp4(n((H, N)) / np.sqrt(H) / u[:, None])
    packed_w3 = pack_fp4(n((H, N)) / np.sqrt(H) / u[:, None])
    return {
        "x_words": packed_xT[0],
        "x_scales": packed_xT[1],
        "w1_words": packed_w1[0],
        "w1_scales": packed_w1[1],
        "gn": (np.random.uniform(0.5, 1.5, (H, 1)) * u[:, None]).astype(np.float32),
        "w2_words": packed_w2[0],
        "w2_scales": packed_w2[1],
        "gm": (np.random.uniform(0.5, 1.5, (H, 1)) * u[:, None]).astype(np.float32),
        "w3_words": packed_w3[0],
        "w3_scales": packed_w3[1],
        "offs": striped(np.random.permutation(T)[:S]),
        "n1": striped8(np.stack([np.random.permutation(S) for _ in range(8)])),
        "n2": striped8(np.stack([np.random.permutation(S) for _ in range(8)])),
        "n3": striped8(np.stack([np.random.permutation(S) for _ in range(8)])),
        "n4": striped8(np.stack([np.random.permutation(S) for _ in range(8)])),
        "n5": striped8(np.stack([np.random.permutation(S) for _ in range(8)])),
        "n6": striped8(np.stack([np.random.permutation(S) for _ in range(8)])),
    }


def reference(x_words, x_scales, w1_words, w1_scales, gn, w2_words, w2_scales, gm, w3_words, w3_scales, offs, n1, n2, n3, n4, n5, n6):
    xq = unpack_weight(x_words, x_scales)[:, unstriped(offs)]
    y = unpack_fp4(w1_words, w1_scales).T @ xq
    z = f64(gn) * (0.75 * ((y - (y[np.arange(H)[:, None], runs(n1, H)])) * (y - (y[np.arange(H)[:, None], runs(n2, H)]))))
    a = unpack_fp4(w2_words, w2_scales).T @ mxq(z, 0, "e4m3")
    z2 = f64(gm) * ((np.tanh(y[np.arange(H)[:, None], runs(n3, H)] - y)) * (y[np.arange(H)[:, None], runs(n4, H)]))
    b = unpack_fp4(w3_words, w3_scales).T @ mxq(z2, 0, "e4m3")
    out_0 = a + (sigmoid(b[np.arange(N)[:, None], runs(n6, N)] - b)) * (a[np.arange(N)[:, None], runs(n5, N)] - a)
    return (out_0,) + planes(out_0)

@@ -1,0 +1,236 @@
+from contextlib import ExitStack
+
+import concourse.mybir as mybir
+
+K, T, S, N, H = 512, 2048, 512, 512, 512
+FLOPS = 2 * K * H * S + 2 * 2 * H * N * S
+
+F32 = mybir.dt.float32
+BF16 = mybir.dt.bfloat16
+I32 = mybir.dt.int32
+U32 = mybir.dt.uint32
+U16 = mybir.dt.uint16
+U8 = mybir.dt.uint8
+FP8X4 = mybir.dt.float8_e4m3fn_x4
+FP4X4 = mybir.dt.float4_e2m1fn_x4
+ALU = mybir.AluOpType
+ACT = mybir.ActivationFunctionType
+
+P = 128
+PACK = 4
+CHUNKS = ((0, 256), (256, 384), (384, 512))
+
+
+def tile_picked_forkpullbquadfdif_none_po_kernel(
+    tc, x_words, x_scales, w1_words, w1_scales, gn, w2_words, w2_scales, gm, w3_words, w3_scales,
+    offs, n1, n2, n3, n4, n5, n6, out_0, out_1, out_2,
+):
+    nc = tc.nc
+    with ExitStack() as ctx:
+        sb = ctx.enter_context(tc.tile_pool(name="sb", bufs=1))
+        psum = ctx.enter_context(tc.psum_pool(name="psum", bufs=1))
+
+        def load_list(name, src):
+            tile = sb.tile([P, S // 16], U16, name=name)
+            nc.sync.dma_start(tile[:], src)
+            return tile
+
+        def load_scale_rows(queues, tile, src):
+            for q in range(4):
+                queues[q].dma_start(
+                    out=tile[32 * q : 32 * q + 4, :].bitcast(I32),
+                    in_=src[0, 4 * q : 4 * q + 4, :].bitcast(I32),
+                )
+
+        def load_words(name, src):
+            tile = sb.tile([P, 2 * N], U8, name=name, align_bytes=64)
+            nc.sync.dma_start(out=tile[:].bitcast(I32), in_=src[0].bitcast(I32))
+            return tile
+
+        def deal(engine, name, raw_words, raw_scales):
+            words = sb.tile([P, 2 * N], U8, name=name + "_words", align_bytes=64)
+            scales = sb.tile([P, N], U8, name=name + "_scales", align_bytes=64)
+            engine.tensor_copy(
+                out=words[:].rearrange("p (t m b) -> p t m b", t=PACK, b=2),
+                in_=raw_words[:].rearrange("p (m t b) -> p t m b", t=PACK, b=2),
+            )
+            engine.tensor_copy(
+                out=scales[:].rearrange("p (t m) -> p t m", t=PACK),
+                in_=raw_scales.rearrange("p (m t) -> p t m", t=PACK),
+            )
+            return words, scales
+
+        def product(bank, weights, t, codes, scales):
+            acc = psum.tile([P, S], F32, name="bank%d" % bank)
+            nc.tensor.matmul_mx(
+                out=acc[:],
+                lhsT=weights[0][:, 2 * P * t : 2 * P * (t + 1)].bitcast(FP4X4),
+                lhsT_scale=weights[1][:, P * t : P * (t + 1)],
+                rhs=codes[:].bitcast(FP8X4),
+                rhs_scale=scales[:],
+                start=True,
+                stop=True,
+            )
+            return acc
+
+        xs_all = sb.tile([P, T], U8, name="xs_all", align_bytes=64)
+        w1s_raw, w2s_raw, w3s_raw = [
+            sb.tile([P, N], U8, name="w%ds_raw" % i, align_bytes=64)[:] for i in (1, 2, 3)
+        ]
+        nc.vector.memset(xs_all[:].bitcast(I32), 0)
+        nc.gpsimd.memset(w1s_raw.bitcast(I32), 0)
+        nc.vector.memset(w3s_raw.bitcast(I32), 0)
+        nc.vector.memset(w2s_raw.bitcast(I32), 0)
+
+        offs_t = load_list("offs_t", offs)
+        w1w_raw = load_words("w1w_raw", w1_words)
+        xw_all = sb.tile([P, T], U32, name="xw_all", align_bytes=64)
+        nc.sync.dma_start(
+            out=xw_all[:].bitcast(I32), in_=x_words[0].rearrange("p n t -> p (n t)").bitcast(I32)
+        )
+        load_scale_rows([nc.sync] * 4, xs_all[:], x_scales)
+        load_scale_rows([nc.sync, nc.sync, nc.sync, nc.gpsimd], w1s_raw, w1_scales)
+        w3w_raw = load_words("w3w_raw", w3_words)
+        w2w_raw = load_words("w2w_raw", w2_words)
+        n3_t = load_list("n3_t", n3)
+        n1_t = load_list("n1_t", n1)
+        load_scale_rows([nc.sync] * 4, w3s_raw, w3_scales)
+        load_scale_rows([nc.sync] * 4, w2s_raw, w2_scales)
+        gm_t = sb.tile([P, PACK], F32, name="gm_t")
+        nc.sync.dma_start(out=gm_t[:], in_=gm.rearrange("(p t) o -> p (t o)", t=PACK))
+        gn_t = sb.tile([P, PACK], F32, name="gn_t")
+        nc.sync.dma_start(out=gn_t[:], in_=gn.rearrange("(p t) o -> p (t o)", t=PACK))
+        n4_t = load_list("n4_t", n4)
+        n2_t = load_list("n2_t", n2)
+        n6_t = load_list("n6_t", n6)
+        n5_t = load_list("n5_t", n5)
+
+        y_win = [sb.tile([P, 2 * S], F32, name="y_win%d" % t) for t in range(PACK)]
+        g_win = [sb.tile([P, 2 * S], F32, name="g_win%d" % t) for t in range(PACK)]
+        for t in range(PACK):
+            nc.vector.memset(y_win[t][:, S:], 0.0)
+
+        w1 = deal(nc.vector, "w1", w1w_raw, w1s_raw)
+
+        xw = sb.tile([P, S], U32, name="xw", align_bytes=64)
+        xs = sb.tile([P, S], U8, name="xs", align_bytes=64)
+        nc.vector.tensor_copy(out=xs[:], in_=xs_all[:].indirect(offs_t[:]))
+        nc.vector.tensor_copy(out=xw[:], in_=xw_all[:].indirect(offs_t[:]))
+
+        y_ps = [product(t, w1, t, xw, xs) for t in range(PACK)]
+
+        gn75 = sb.tile([P, PACK], F32, name="gn75")
+        nc.vector.tensor_scalar(out=gn75[:], in0=gn_t[:], scalar1=0.75, scalar2=None, op0=ALU.mult)
+        w3 = deal(nc.vector, "w3", w3w_raw, w3s_raw)
+        w2 = deal(nc.vector, "w2", w2w_raw, w2s_raw)
+
+        d1 = sb.tile([P, PACK, S], F32, name="d1")
+        d3 = sb.tile([P, PACK, S], F32, name="d3")
+        z2f = sb.tile([P, PACK, S], F32, name="z2f")
+        for t in range(PACK):
+            nc.scalar.copy(out=y_win[t][:, :S], in_=y_ps[t][:])
+            nc.scalar.copy(out=g_win[t][:, S:], in_=y_ps[t][:])
+            nc.vector.tensor_tensor(d3[:, t, :], y_win[t][:].indirect(n3_t[:]), g_win[t][:, S:], ALU.subtract)
+            nc.vector.tensor_tensor(d1[:, t, :], y_win[t][:].indirect(n1_t[:]), g_win[t][:, S:], ALU.subtract)
+        for t in range(PACK):
+            nc.scalar.activation(out=d3[:, t, :], in_=d3[:, t, :], func=ACT.Tanh)
+            nc.scalar.activation(out=g_win[t][:, :S], in_=y_ps[t][:], func=ACT.Copy, scale=gm_t[:, t : t + 1])
+        for t in range(PACK):
+            nc.vector.tensor_tensor(z2f[:, t, :], g_win[t][:].indirect(n4_t[:]), d3[:, t, :], ALU.mult)
+            nc.scalar.activation(out=d1[:, t, :], in_=d1[:, t, :], func=ACT.Copy, scale=gn75[:, t : t + 1])
+
+        zb = sb.tile([P, S * PACK], BF16, name="zb", align_bytes=64)
+        nc.scalar.activation(
+            out=zb[:].rearrange("p (c i t) -> p c t i", i=4, t=PACK),
+            in_=z2f[:].rearrange("p t (c i) -> p c t i", i=4),
+            func=ACT.Copy,
+        )
+        d2 = d3
+        for t in range(2):
+            nc.vector.tensor_tensor(d2[:, t, :], y_win[t][:].indirect(n2_t[:]), g_win[t][:, S:], ALU.subtract)
+        z2_codes = sb.tile([P, S], U32, name="z2_codes", align_bytes=64)
+        z2_scales = sb.tile([P, S], U8, name="z2_scales", align_bytes=64)
+        nc.vector.quantize_mx(out=z2_codes[:].bitcast(FP8X4), scales=z2_scales[:], in_=zb[:])
+        b_ps = [product(PACK + t, w3, t, z2_codes, z2_scales) for t in range(PACK)]
+        for t in range(2, PACK):
+            nc.vector.tensor_tensor(d2[:, t, :], y_win[t][:].indirect(n2_t[:]), g_win[t][:, S:], ALU.subtract)
+        b_plain = sb.tile([P, PACK, S], F32, name="b_plain")
+        for t in range(PACK):
+            nc.scalar.copy(out=g_win[t][:, :S], in_=b_ps[t][:])
+            nc.scalar.copy(out=b_plain[:, t, :], in_=b_ps[t][:])
+
+        nc.vector.tensor_tensor(
+            zb[:].rearrange("p (c i t) -> p c t i", i=2, t=PACK),
+            d1[:].rearrange("p t (c i) -> p c t i", i=2),
+            d2[:].rearrange("p t (c i) -> p c t i", i=2),
+            ALU.mult,
+        )
+        gate = sb.tile([P, PACK, S], F32, name="gate")
+        z_codes = sb.tile([P, S], U32, name="z_codes", align_bytes=64)
+        z_scales = sb.tile([P, S], U8, name="z_scales", align_bytes=64)
+        nc.vector.tensor_tensor(gate[:, 0, :], g_win[0][:].indirect(n6_t[:]), b_plain[:, 0, :], ALU.subtract)
+        nc.vector.quantize_mx(out=z_codes[:].bitcast(FP8X4), scales=z_scales[:], in_=zb[:])
+        a_ps = [product(t, w2, t, z_codes, z_scales) for t in range(PACK)]
+        for t in range(1, PACK):
+            nc.vector.tensor_tensor(gate[:, t, :], g_win[t][:].indirect(n6_t[:]), b_plain[:, t, :], ALU.subtract)
+        a_win = [sb.tile([P, S], F32, name="a_win%d" % t) for t in range(PACK)]
+        for t in range(PACK):
+            nc.scalar.activation(out=gate[:, t, :], in_=gate[:, t, :], func=ACT.Sigmoid)
+            nc.scalar.copy(out=a_win[t][:], in_=a_ps[t][:])
+
+        rest = z2f
+        o_codes = sb.tile([P, S], U32, name="o_codes", align_bytes=64)
+        o_scales = sb.tile([P, S], U8, name="o_scales", align_bytes=64)
+        out_rows = out_0.rearrange("(p t) j -> p t j", t=PACK)
+        out_words = out_1[0].rearrange("p n t -> p (n t)").bitcast(I32)
+
+        def pull(c, t, pulled):
+            lo, hi = CHUNKS[c]
+            nc.vector.tensor_tensor(
+                pulled[:, t, :], a_win[t][:].indirect(n5_t[:, lo // 16 : hi // 16]), gate[:, t, lo:hi], ALU.mult
+            )
+
+        def join(c, pulled):
+            lo, hi = CHUNKS[c]
+            res = sb.tile([P, PACK, hi - lo], F32, name="res%d" % c)
+            nc.vector.tensor_tensor(res[:], pulled[:], rest[:, :, lo:hi], ALU.subtract)
+            nc.sync.dma_start(out=out_rows[:, :, lo:hi], in_=res[:])
+            rounded = sb.tile([P, PACK * (hi - lo)], BF16, name="rounded%d" % c, align_bytes=64)
+            dst = rounded[:].rearrange("p (c i t) -> p c t i", i=4, t=PACK)
+            src = res[:].rearrange("p t (c i) -> p c t i", i=4)
+            if c == len(CHUNKS) - 1:
+                nc.vector.tensor_copy(out=dst, in_=src)
+            else:
+                nc.scalar.activation(out=dst, in_=src, func=ACT.Copy)
+            return rounded
+
+        def quantise(c, rounded):
+            lo, hi = CHUNKS[c]
+            nc.vector.quantize_mx(out=o_codes[:, lo:hi].bitcast(FP8X4), scales=o_scales[:, lo:hi], in_=rounded[:])
+            nc.scalar.dma_start(out=out_words[:, lo:hi], in_=o_codes[:, lo:hi].bitcast(I32))
+
+        pulled = [sb.tile([P, PACK, hi - lo], F32, name="pulled%d" % c) for c, (lo, hi) in enumerate(CHUNKS)]
+        for t in range(PACK):
+            nc.vector.scalar_tensor_tensor(
+                out=rest[:, t, :], in0=gate[:, t, :], scalar=1.0, in1=a_win[t][:], op0=ALU.subtract, op1=ALU.mult
+            )
+            pull(0, t, pulled[0])
+        pull(1, 0, pulled[1])
+        r0 = join(0, pulled[0])
+        for t in range(1, PACK):
+            pull(1, t, pulled[1])
+        pull(2, 0, pulled[2])
+        r1 = join(1, pulled[1])
+        pull(2, 1, pulled[2])
+        quantise(0, r0)
+        pull(2, 2, pulled[2])
+        pull(2, 3, pulled[2])
+        quantise(1, r1)
+        r2 = join(2, pulled[2])
+        quantise(2, r2)
+        for q in range(4):
+            queue = nc.sync if q % 2 == 0 else nc.scalar
+            queue.dma_start(
+                out=out_2[0, 4 * q : 4 * q + 4, :].bitcast(I32),
+                in_=o_scales[32 * q : 32 * q + 4, :].bitcast(I32),
+            )

@@ -35,9 +35,9 @@ def tile_picked_forkpullbquadfdif_none_po_kernel(
             nc.sync.dma_start(tile[:], src)
             return tile
 
-        def load_scale_rows(queues, tile, src):
+        def load_scale_rows(tile, src):
             for q in range(4):
-                queues[q].dma_start(
+                nc.sync.dma_start(
                     out=tile[32 * q : 32 * q + 4, :].bitcast(I32),
                     in_=src[0, 4 * q : 4 * q + 4, :].bitcast(I32),
                 )
@@ -47,94 +47,109 @@ def tile_picked_forkpullbquadfdif_none_po_kernel(
             nc.sync.dma_start(out=tile[:].bitcast(I32), in_=src[0].bitcast(I32))
             return tile
 
-        def deal(engine, name, raw_words, raw_scales):
+        def deal(name, raw_words, raw_scales):
             words = sb.tile([P, 2 * N], U8, name=name + "_words", align_bytes=64)
             scales = sb.tile([P, N], U8, name=name + "_scales", align_bytes=64)
-            engine.tensor_copy(
+            nc.vector.tensor_copy(
                 out=words[:].rearrange("p (t m b) -> p t m b", t=PACK, b=2),
                 in_=raw_words[:].rearrange("p (m t b) -> p t m b", t=PACK, b=2),
             )
-            engine.tensor_copy(
+            nc.vector.tensor_copy(
                 out=scales[:].rearrange("p (t m) -> p t m", t=PACK),
                 in_=raw_scales.rearrange("p (m t) -> p t m", t=PACK),
             )
             return words, scales
 
-        def product(bank, weights, t, codes, scales):
-            acc = psum.tile([P, S], F32, name="bank%d" % bank)
+        def bank(index):
+            return psum.tile([P, S], F32, name="bank%d" % index)
+
+        def product(acc, weights, t, codes, scales):
             nc.tensor.matmul_mx(
-                out=acc[:],
+                out=acc,
                 lhsT=weights[0][:, 2 * P * t : 2 * P * (t + 1)].bitcast(FP4X4),
                 lhsT_scale=weights[1][:, P * t : P * (t + 1)],
-                rhs=codes[:].bitcast(FP8X4),
-                rhs_scale=scales[:],
+                rhs=codes.bitcast(FP8X4),
+                rhs_scale=scales,
                 start=True,
                 stop=True,
             )
-            return acc
 
         xs_all = sb.tile([P, T], U8, name="xs_all", align_bytes=64)
-        w1s_raw, w2s_raw, w3s_raw = [
-            sb.tile([P, N], U8, name="w%ds_raw" % i, align_bytes=64)[:] for i in (1, 2, 3)
-        ]
-        nc.vector.memset(xs_all[:].bitcast(I32), 0)
+        w1s_raw = sb.tile([P, H], U8, name="w1s_raw", tag="w1s_then_xw1", align_bytes=64)[:]
+        w2s_raw, w3s_raw = [sb.tile([P, N], U8, name="w%ds_raw" % i, align_bytes=64)[:] for i in (2, 3)]
+        nc.gpsimd.memset(xs_all[:].bitcast(I32), 0)
         nc.gpsimd.memset(w1s_raw.bitcast(I32), 0)
-        nc.vector.memset(w3s_raw.bitcast(I32), 0)
-        nc.vector.memset(w2s_raw.bitcast(I32), 0)
+        nc.gpsimd.memset(w3s_raw.bitcast(I32), 0)
+        nc.gpsimd.memset(w2s_raw.bitcast(I32), 0)
+
+        def load_gain(name, src):
+            tile = sb.tile([P, PACK], F32, name=name)
+            nc.sync.dma_start(out=tile[:], in_=src.rearrange("(p t) o -> p (t o)", t=PACK))
+            return tile
 
         offs_t = load_list("offs_t", offs)
         w1w_raw = load_words("w1w_raw", w1_words)
+        load_scale_rows(xs_all[:], x_scales)
         xw_all = sb.tile([P, T], U32, name="xw_all", align_bytes=64)
         nc.sync.dma_start(
             out=xw_all[:].bitcast(I32), in_=x_words[0].rearrange("p n t -> p (n t)").bitcast(I32)
         )
-        load_scale_rows([nc.sync] * 4, xs_all[:], x_scales)
-        load_scale_rows([nc.sync, nc.sync, nc.sync, nc.gpsimd], w1s_raw, w1_scales)
+        load_scale_rows(w1s_raw, w1_scales)
+        n3_t = load_list("n3_t", n3)
         w3w_raw = load_words("w3w_raw", w3_words)
         w2w_raw = load_words("w2w_raw", w2_words)
-        n3_t = load_list("n3_t", n3)
         n1_t = load_list("n1_t", n1)
-        load_scale_rows([nc.sync] * 4, w3s_raw, w3_scales)
-        load_scale_rows([nc.sync] * 4, w2s_raw, w2_scales)
-        gm_t = sb.tile([P, PACK], F32, name="gm_t")
-        nc.sync.dma_start(out=gm_t[:], in_=gm.rearrange("(p t) o -> p (t o)", t=PACK))
-        gn_t = sb.tile([P, PACK], F32, name="gn_t")
-        nc.sync.dma_start(out=gn_t[:], in_=gn.rearrange("(p t) o -> p (t o)", t=PACK))
+        gm_t = load_gain("gm_t", gm)
+        load_scale_rows(w3s_raw, w3_scales)
+        gn_t = load_gain("gn_t", gn)
         n4_t = load_list("n4_t", n4)
+        load_scale_rows(w2s_raw, w2_scales)
         n2_t = load_list("n2_t", n2)
         n6_t = load_list("n6_t", n6)
         n5_t = load_list("n5_t", n5)
 
         y_win = [sb.tile([P, 2 * S], F32, name="y_win%d" % t) for t in range(PACK)]
         g_win = [sb.tile([P, 2 * S], F32, name="g_win%d" % t) for t in range(PACK)]
-        for t in range(PACK):
-            nc.vector.memset(y_win[t][:, S:], 0.0)
 
-        w1 = deal(nc.vector, "w1", w1w_raw, w1s_raw)
+        w1 = deal("w1", w1w_raw, w1s_raw)
 
-        xw = sb.tile([P, S], U32, name="xw", align_bytes=64)
         xs = sb.tile([P, S], U8, name="xs", align_bytes=64)
         nc.vector.tensor_copy(out=xs[:], in_=xs_all[:].indirect(offs_t[:]))
-        nc.vector.tensor_copy(out=xw[:], in_=xw_all[:].indirect(offs_t[:]))
-
-        y_ps = [product(t, w1, t, xw, xs) for t in range(PACK)]
+        halves = (slice(0, S // 2), slice(S // 2, S))
+        y_ps = [bank(t) for t in range(PACK)]
+        y0_ps = (y_ps[0], bank(7))
+        xw = []
+        for h, cols in enumerate(halves):
+            half = sb.tile([P, S // 2], U32, name="xw%d" % h, tag=("xw0", "w1s_then_xw1")[h], align_bytes=64)
+            entries = offs_t[:, cols.start // 16 : cols.stop // 16]
+            nc.vector.tensor_copy(out=half[:], in_=xw_all[:].indirect(entries))
+            product(y0_ps[h][:, cols], w1, 0, half[:], xs[:, cols])
+            xw.append(half)
+        for t in range(1, PACK):
+            for h, cols in enumerate(halves):
+                product(y_ps[t][:, cols], w1, t, xw[h][:], xs[:, cols])
 
         gn75 = sb.tile([P, PACK], F32, name="gn75")
         nc.vector.tensor_scalar(out=gn75[:], in0=gn_t[:], scalar1=0.75, scalar2=None, op0=ALU.mult)
-        w3 = deal(nc.vector, "w3", w3w_raw, w3s_raw)
-        w2 = deal(nc.vector, "w2", w2w_raw, w2s_raw)
+        w3 = deal("w3", w3w_raw, w3s_raw)
+        w2 = deal("w2", w2w_raw, w2s_raw)
 
         d1 = sb.tile([P, PACK, S], F32, name="d1")
         d3 = sb.tile([P, PACK, S], F32, name="d3")
         z2f = sb.tile([P, PACK, S], F32, name="z2f")
         for t in range(PACK):
-            nc.scalar.copy(out=y_win[t][:, :S], in_=y_ps[t][:])
-            nc.scalar.copy(out=g_win[t][:, S:], in_=y_ps[t][:])
+            if t == 0:
+                for h, cols in enumerate(halves):
+                    nc.scalar.copy(out=y_win[0][:, cols], in_=y0_ps[h][:, cols])
+                    nc.scalar.copy(out=g_win[0][:, S + cols.start : S + cols.stop], in_=y0_ps[h][:, cols])
+            else:
+                nc.scalar.copy(out=y_win[t][:, :S], in_=y_ps[t][:])
+                nc.scalar.copy(out=g_win[t][:, S:], in_=y_ps[t][:])
             nc.vector.tensor_tensor(d3[:, t, :], y_win[t][:].indirect(n3_t[:]), g_win[t][:, S:], ALU.subtract)
             nc.vector.tensor_tensor(d1[:, t, :], y_win[t][:].indirect(n1_t[:]), g_win[t][:, S:], ALU.subtract)
         for t in range(PACK):
             nc.scalar.activation(out=d3[:, t, :], in_=d3[:, t, :], func=ACT.Tanh)
-            nc.scalar.activation(out=g_win[t][:, :S], in_=y_ps[t][:], func=ACT.Copy, scale=gm_t[:, t : t + 1])
+            nc.scalar.activation(out=g_win[t][:, :S], in_=y_win[t][:, :S], func=ACT.Copy, scale=gm_t[:, t : t + 1])
         for t in range(PACK):
             nc.vector.tensor_tensor(z2f[:, t, :], g_win[t][:].indirect(n4_t[:]), d3[:, t, :], ALU.mult)
             nc.scalar.activation(out=d1[:, t, :], in_=d1[:, t, :], func=ACT.Copy, scale=gn75[:, t : t + 1])
@@ -151,7 +166,9 @@ def tile_picked_forkpullbquadfdif_none_po_kernel(
         z2_codes = sb.tile([P, S], U32, name="z2_codes", align_bytes=64)
         z2_scales = sb.tile([P, S], U8, name="z2_scales", align_bytes=64)
         nc.vector.quantize_mx(out=z2_codes[:].bitcast(FP8X4), scales=z2_scales[:], in_=zb[:])
-        b_ps = [product(PACK + t, w3, t, z2_codes, z2_scales) for t in range(PACK)]
+        b_ps = [bank(PACK + t) for t in range(PACK)]
+        for t in range(PACK):
+            product(b_ps[t][:], w3, t, z2_codes[:], z2_scales[:])
         for t in range(2, PACK):
             nc.vector.tensor_tensor(d2[:, t, :], y_win[t][:].indirect(n2_t[:]), g_win[t][:, S:], ALU.subtract)
         b_plain = sb.tile([P, PACK, S], F32, name="b_plain")
@@ -170,7 +187,9 @@ def tile_picked_forkpullbquadfdif_none_po_kernel(
         z_scales = sb.tile([P, S], U8, name="z_scales", align_bytes=64)
         nc.vector.tensor_tensor(gate[:, 0, :], g_win[0][:].indirect(n6_t[:]), b_plain[:, 0, :], ALU.subtract)
         nc.vector.quantize_mx(out=z_codes[:].bitcast(FP8X4), scales=z_scales[:], in_=zb[:])
-        a_ps = [product(t, w2, t, z_codes, z_scales) for t in range(PACK)]
+        a_ps = [bank(t) for t in range(PACK)]
+        for t in range(PACK):
+            product(a_ps[t][:], w2, t, z_codes[:], z_scales[:])
         for t in range(1, PACK):
             nc.vector.tensor_tensor(gate[:, t, :], g_win[t][:].indirect(n6_t[:]), b_plain[:, t, :], ALU.subtract)
         a_win = [sb.tile([P, S], F32, name="a_win%d" % t) for t in range(PACK)]
@@ -207,7 +226,8 @@ def tile_picked_forkpullbquadfdif_none_po_kernel(
         def quantise(c, rounded):
             lo, hi = CHUNKS[c]
             nc.vector.quantize_mx(out=o_codes[:, lo:hi].bitcast(FP8X4), scales=o_scales[:, lo:hi], in_=rounded[:])
-            nc.scalar.dma_start(out=out_words[:, lo:hi], in_=o_codes[:, lo:hi].bitcast(I32))
+            queue = nc.scalar if c == len(CHUNKS) - 1 else nc.sync
+            queue.dma_start(out=out_words[:, lo:hi], in_=o_codes[:, lo:hi].bitcast(I32))
 
         pulled = [sb.tile([P, PACK, hi - lo], F32, name="pulled%d" % c) for c, (lo, hi) in enumerate(CHUNKS)]
         for t in range(PACK):

@@ -47,10 +47,10 @@ def tile_picked_forkpullbquadfdif_none_po_kernel(
             nc.sync.dma_start(out=tile[:].bitcast(I32), in_=src[0].bitcast(I32))
             return tile
 
-        def deal(name, raw_words, raw_scales):
+        def deal(engine, name, raw_words, raw_scales):
             words = sb.tile([P, 2 * N], U8, name=name + "_words", align_bytes=64)
             scales = sb.tile([P, N], U8, name=name + "_scales", align_bytes=64)
-            nc.vector.tensor_copy(
+            engine.tensor_copy(
                 out=words[:].rearrange("p (t m b) -> p t m b", t=PACK, b=2),
                 in_=raw_words[:].rearrange("p (m t b) -> p t m b", t=PACK, b=2),
             )
@@ -76,7 +76,8 @@ def tile_picked_forkpullbquadfdif_none_po_kernel(
 
         xs_all = sb.tile([P, T], U8, name="xs_all", align_bytes=64)
         w1s_raw = sb.tile([P, H], U8, name="w1s_raw", tag="w1s_then_xw1", align_bytes=64)[:]
-        w2s_raw, w3s_raw = [sb.tile([P, N], U8, name="w%ds_raw" % i, align_bytes=64)[:] for i in (2, 3)]
+        w2s_raw = sb.tile([P, N], U8, name="w2s_raw", tag="w2s_then_d3", align_bytes=64)[:]
+        w3s_raw = sb.tile([P, N], U8, name="w3s_raw", align_bytes=64)[:]
         nc.gpsimd.memset(xs_all[:].bitcast(I32), 0)
         nc.gpsimd.memset(w1s_raw.bitcast(I32), 0)
         nc.gpsimd.memset(w3s_raw.bitcast(I32), 0)
@@ -95,15 +96,15 @@ def tile_picked_forkpullbquadfdif_none_po_kernel(
             out=xw_all[:].bitcast(I32), in_=x_words[0].rearrange("p n t -> p (n t)").bitcast(I32)
         )
         load_scale_rows(w1s_raw, w1_scales)
-        n3_t = load_list("n3_t", n3)
         w3w_raw = load_words("w3w_raw", w3_words)
         w2w_raw = load_words("w2w_raw", w2_words)
+        n3_t = load_list("n3_t", n3)
+        load_scale_rows(w3s_raw, w3_scales)
+        load_scale_rows(w2s_raw, w2_scales)
         n1_t = load_list("n1_t", n1)
         gm_t = load_gain("gm_t", gm)
-        load_scale_rows(w3s_raw, w3_scales)
         gn_t = load_gain("gn_t", gn)
         n4_t = load_list("n4_t", n4)
-        load_scale_rows(w2s_raw, w2_scales)
         n2_t = load_list("n2_t", n2)
         n6_t = load_list("n6_t", n6)
         n5_t = load_list("n5_t", n5)
@@ -111,7 +112,7 @@ def tile_picked_forkpullbquadfdif_none_po_kernel(
         y_win = [sb.tile([P, 2 * S], F32, name="y_win%d" % t) for t in range(PACK)]
         g_win = [sb.tile([P, 2 * S], F32, name="g_win%d" % t) for t in range(PACK)]
 
-        w1 = deal("w1", w1w_raw, w1s_raw)
+        w1 = deal(nc.vector, "w1", w1w_raw, w1s_raw)
 
         xs = sb.tile([P, S], U8, name="xs", align_bytes=64)
         nc.vector.tensor_copy(out=xs[:], in_=xs_all[:].indirect(offs_t[:]))
@@ -130,12 +131,12 @@ def tile_picked_forkpullbquadfdif_none_po_kernel(
                 product(y_ps[t][:, cols], w1, t, xw[h][:], xs[:, cols])
 
         gn75 = sb.tile([P, PACK], F32, name="gn75")
-        nc.vector.tensor_scalar(out=gn75[:], in0=gn_t[:], scalar1=0.75, scalar2=None, op0=ALU.mult)
-        w3 = deal("w3", w3w_raw, w3s_raw)
-        w2 = deal("w2", w2w_raw, w2s_raw)
+        nc.scalar.activation(out=gn75[:], in_=gn_t[:], func=ACT.Copy, scale=0.75)
+        w3 = deal(nc.gpsimd, "w3", w3w_raw, w3s_raw)
+        w2 = deal(nc.gpsimd, "w2", w2w_raw, w2s_raw)
 
         d1 = sb.tile([P, PACK, S], F32, name="d1")
-        d3 = sb.tile([P, PACK, S], F32, name="d3")
+        d3 = sb.tile([P, PACK, S], F32, name="d3", tag="w2s_then_d3", align_bytes=64)
         z2f = sb.tile([P, PACK, S], F32, name="z2f")
         for t in range(PACK):
             if t == 0:
@@ -214,6 +215,10 @@ def tile_picked_forkpullbquadfdif_none_po_kernel(
             res = sb.tile([P, PACK, hi - lo], F32, name="res%d" % c)
             nc.vector.tensor_tensor(res[:], pulled[:], rest[:, :, lo:hi], ALU.subtract)
             nc.sync.dma_start(out=out_rows[:, :, lo:hi], in_=res[:])
+            return res
+
+        def interleave(c, res):
+            lo, hi = CHUNKS[c]
             rounded = sb.tile([P, PACK * (hi - lo)], BF16, name="rounded%d" % c, align_bytes=64)
             dst = rounded[:].rearrange("p (c i t) -> p c t i", i=4, t=PACK)
             src = res[:].rearrange("p t (c i) -> p c t i", i=4)
@@ -236,18 +241,17 @@ def tile_picked_forkpullbquadfdif_none_po_kernel(
             )
             pull(0, t, pulled[0])
         pull(1, 0, pulled[1])
-        r0 = join(0, pulled[0])
+        r0 = interleave(0, join(0, pulled[0]))
         for t in range(1, PACK):
             pull(1, t, pulled[1])
         pull(2, 0, pulled[2])
-        r1 = join(1, pulled[1])
-        pull(2, 1, pulled[2])
+        r1 = interleave(1, join(1, pulled[1]))
+        for t in range(1, PACK):
+            pull(2, t, pulled[2])
         quantise(0, r0)
-        pull(2, 2, pulled[2])
-        pull(2, 3, pulled[2])
+        res2 = join(2, pulled[2])
         quantise(1, r1)
-        r2 = join(2, pulled[2])
-        quantise(2, r2)
+        quantise(2, interleave(2, res2))
         for q in range(4):
             queue = nc.sync if q % 2 == 0 else nc.scalar
             queue.dma_start(

from contextlib import ExitStack

import concourse.mybir as mybir

K, T, S, N, H = 512, 2048, 512, 512, 512
FLOPS = 2 * K * H * S + 2 * 2 * H * N * S

F32 = mybir.dt.float32
BF16 = mybir.dt.bfloat16
I32 = mybir.dt.int32
U32 = mybir.dt.uint32
U16 = mybir.dt.uint16
U8 = mybir.dt.uint8
FP8X4 = mybir.dt.float8_e4m3fn_x4
FP4X4 = mybir.dt.float4_e2m1fn_x4
ALU = mybir.AluOpType
ACT = mybir.ActivationFunctionType

P = 128
PACK = 4
CHUNKS = ((0, 256), (256, 384), (384, 512))


def tile_picked_forkpullbquadfdif_none_po_kernel(
    tc, x_words, x_scales, w1_words, w1_scales, gn, w2_words, w2_scales, gm, w3_words, w3_scales,
    offs, n1, n2, n3, n4, n5, n6, out_0, out_1, out_2,
):
    nc = tc.nc
    with ExitStack() as ctx:
        sb = ctx.enter_context(tc.tile_pool(name="sb", bufs=1))
        psum = ctx.enter_context(tc.psum_pool(name="psum", bufs=1))

        def load_list(name, src):
            tile = sb.tile([P, S // 16], U16, name=name)
            nc.sync.dma_start(tile[:], src)
            return tile

        def load_scale_rows(tile, src):
            for q in range(4):
                nc.sync.dma_start(
                    out=tile[32 * q : 32 * q + 4, :].bitcast(I32),
                    in_=src[0, 4 * q : 4 * q + 4, :].bitcast(I32),
                )

        def load_words(name, src):
            tile = sb.tile([P, 2 * N], U8, name=name, align_bytes=64)
            nc.sync.dma_start(out=tile[:].bitcast(I32), in_=src[0].bitcast(I32))
            return tile

        def deal(engine, name, raw_words, raw_scales):
            words = sb.tile([P, 2 * N], U8, name=name + "_words", align_bytes=64)
            scales = sb.tile([P, N], U8, name=name + "_scales", align_bytes=64)
            engine.tensor_copy(
                out=words[:].rearrange("p (t m b) -> p t m b", t=PACK, b=2),
                in_=raw_words[:].rearrange("p (m t b) -> p t m b", t=PACK, b=2),
            )
            nc.vector.tensor_copy(
                out=scales[:].rearrange("p (t m) -> p t m", t=PACK),
                in_=raw_scales.rearrange("p (m t) -> p t m", t=PACK),
            )
            return words, scales

        def bank(index):
            return psum.tile([P, S], F32, name="bank%d" % index)

        def product(acc, weights, t, codes, scales):
            nc.tensor.matmul_mx(
                out=acc,
                lhsT=weights[0][:, 2 * P * t : 2 * P * (t + 1)].bitcast(FP4X4),
                lhsT_scale=weights[1][:, P * t : P * (t + 1)],
                rhs=codes.bitcast(FP8X4),
                rhs_scale=scales,
                start=True,
                stop=True,
            )

        xs_all = sb.tile([P, T], U8, name="xs_all", align_bytes=64)
        w1s_raw = sb.tile([P, H], U8, name="w1s_raw", tag="w1s_then_xw1", align_bytes=64)[:]
        w2s_raw = sb.tile([P, N], U8, name="w2s_raw", tag="w2s_then_d3", align_bytes=64)[:]
        w3s_raw = sb.tile([P, N], U8, name="w3s_raw", align_bytes=64)[:]
        nc.gpsimd.memset(xs_all[:].bitcast(I32), 0)
        nc.gpsimd.memset(w1s_raw.bitcast(I32), 0)
        nc.gpsimd.memset(w3s_raw.bitcast(I32), 0)
        nc.gpsimd.memset(w2s_raw.bitcast(I32), 0)

        def load_gain(name, src):
            tile = sb.tile([P, PACK], F32, name=name)
            nc.sync.dma_start(out=tile[:], in_=src.rearrange("(p t) o -> p (t o)", t=PACK))
            return tile

        offs_t = load_list("offs_t", offs)
        w1w_raw = load_words("w1w_raw", w1_words)
        load_scale_rows(xs_all[:], x_scales)
        xw_all = sb.tile([P, T], U32, name="xw_all", align_bytes=64)
        nc.sync.dma_start(
            out=xw_all[:].bitcast(I32), in_=x_words[0].rearrange("p n t -> p (n t)").bitcast(I32)
        )
        load_scale_rows(w1s_raw, w1_scales)
        w3w_raw = load_words("w3w_raw", w3_words)
        w2w_raw = load_words("w2w_raw", w2_words)
        n3_t = load_list("n3_t", n3)
        load_scale_rows(w3s_raw, w3_scales)
        load_scale_rows(w2s_raw, w2_scales)
        n1_t = load_list("n1_t", n1)
        gm_t = load_gain("gm_t", gm)
        gn_t = load_gain("gn_t", gn)
        n4_t = load_list("n4_t", n4)
        n2_t = load_list("n2_t", n2)
        n6_t = load_list("n6_t", n6)
        n5_t = load_list("n5_t", n5)

        y_win = [sb.tile([P, 2 * S], F32, name="y_win%d" % t) for t in range(PACK)]
        g_win = [sb.tile([P, 2 * S], F32, name="g_win%d" % t) for t in range(PACK)]

        w1 = deal(nc.vector, "w1", w1w_raw, w1s_raw)

        xs = sb.tile([P, S], U8, name="xs", align_bytes=64)
        nc.vector.tensor_copy(out=xs[:], in_=xs_all[:].indirect(offs_t[:]))
        halves = (slice(0, S // 2), slice(S // 2, S))
        y_ps = [bank(t) for t in range(PACK)]
        y0_ps = (y_ps[0], bank(7))
        xw = []
        for h, cols in enumerate(halves):
            half = sb.tile([P, S // 2], U32, name="xw%d" % h, tag=("xw0", "w1s_then_xw1")[h], align_bytes=64)
            entries = offs_t[:, cols.start // 16 : cols.stop // 16]
            nc.vector.tensor_copy(out=half[:], in_=xw_all[:].indirect(entries))
            product(y0_ps[h][:, cols], w1, 0, half[:], xs[:, cols])
            xw.append(half)
        for t in range(1, PACK):
            for h, cols in enumerate(halves):
                product(y_ps[t][:, cols], w1, t, xw[h][:], xs[:, cols])

        gn75 = sb.tile([P, PACK], F32, name="gn75")
        nc.scalar.activation(out=gn75[:], in_=gn_t[:], func=ACT.Copy, scale=0.75)
        w3 = deal(nc.gpsimd, "w3", w3w_raw, w3s_raw)
        w2 = deal(nc.gpsimd, "w2", w2w_raw, w2s_raw)

        d1 = sb.tile([P, PACK, S], F32, name="d1")
        d3 = sb.tile([P, PACK, S], F32, name="d3", tag="w2s_then_d3", align_bytes=64)
        z2f = sb.tile([P, PACK, S], F32, name="z2f")
        for t in range(PACK):
            if t == 0:
                for h, cols in enumerate(halves):
                    nc.scalar.copy(out=y_win[0][:, cols], in_=y0_ps[h][:, cols])
                    nc.scalar.copy(out=g_win[0][:, S + cols.start : S + cols.stop], in_=y0_ps[h][:, cols])
            else:
                nc.scalar.copy(out=y_win[t][:, :S], in_=y_ps[t][:])
                nc.scalar.copy(out=g_win[t][:, S:], in_=y_ps[t][:])
            nc.vector.tensor_tensor(d3[:, t, :], y_win[t][:].indirect(n3_t[:]), g_win[t][:, S:], ALU.subtract)
            nc.vector.tensor_tensor(d1[:, t, :], y_win[t][:].indirect(n1_t[:]), g_win[t][:, S:], ALU.subtract)
        for t in range(PACK):
            nc.scalar.activation(out=d3[:, t, :], in_=d3[:, t, :], func=ACT.Tanh)
            nc.scalar.activation(out=g_win[t][:, :S], in_=y_win[t][:, :S], func=ACT.Copy, scale=gm_t[:, t : t + 1])
        for t in range(PACK):
            nc.vector.tensor_tensor(z2f[:, t, :], g_win[t][:].indirect(n4_t[:]), d3[:, t, :], ALU.mult)
            nc.scalar.activation(out=d1[:, t, :], in_=d1[:, t, :], func=ACT.Copy, scale=gn75[:, t : t + 1])

        zb = sb.tile([P, S * PACK], BF16, name="zb", align_bytes=64)
        nc.scalar.activation(
            out=zb[:].rearrange("p (c i t) -> p c t i", i=4, t=PACK),
            in_=z2f[:].rearrange("p t (c i) -> p c t i", i=4),
            func=ACT.Copy,
        )
        d2 = d3
        for t in range(2):
            nc.vector.tensor_tensor(d2[:, t, :], y_win[t][:].indirect(n2_t[:]), g_win[t][:, S:], ALU.subtract)
        z2_codes = sb.tile([P, S], U32, name="z2_codes", align_bytes=64)
        z2_scales = sb.tile([P, S], U8, name="z2_scales", align_bytes=64)
        nc.vector.quantize_mx(out=z2_codes[:].bitcast(FP8X4), scales=z2_scales[:], in_=zb[:])
        b_ps = [bank(PACK + t) for t in range(PACK)]
        for t in range(PACK):
            product(b_ps[t][:], w3, t, z2_codes[:], z2_scales[:])
        for t in range(2, PACK):
            nc.vector.tensor_tensor(d2[:, t, :], y_win[t][:].indirect(n2_t[:]), g_win[t][:, S:], ALU.subtract)
        b_plain = sb.tile([P, PACK, S], F32, name="b_plain")
        for t in range(PACK):
            nc.scalar.copy(out=g_win[t][:, :S], in_=b_ps[t][:])
            nc.scalar.copy(out=b_plain[:, t, :], in_=b_ps[t][:])

        nc.vector.tensor_tensor(
            zb[:].rearrange("p (c i t) -> p c t i", i=2, t=PACK),
            d1[:].rearrange("p t (c i) -> p c t i", i=2),
            d2[:].rearrange("p t (c i) -> p c t i", i=2),
            ALU.mult,
        )
        gate = sb.tile([P, PACK, S], F32, name="gate")
        z_codes = sb.tile([P, S], U32, name="z_codes", align_bytes=64)
        z_scales = sb.tile([P, S], U8, name="z_scales", align_bytes=64)
        nc.vector.tensor_tensor(gate[:, 0, :], g_win[0][:].indirect(n6_t[:]), b_plain[:, 0, :], ALU.subtract)
        nc.vector.quantize_mx(out=z_codes[:].bitcast(FP8X4), scales=z_scales[:], in_=zb[:])
        a_ps = [bank(t) for t in range(PACK)]
        for t in range(PACK):
            product(a_ps[t][:], w2, t, z_codes[:], z_scales[:])
        for t in range(1, PACK):
            nc.vector.tensor_tensor(gate[:, t, :], g_win[t][:].indirect(n6_t[:]), b_plain[:, t, :], ALU.subtract)
        a_win = [sb.tile([P, S], F32, name="a_win%d" % t) for t in range(PACK)]
        for t in range(PACK):
            nc.scalar.activation(out=gate[:, t, :], in_=gate[:, t, :], func=ACT.Sigmoid)
            nc.scalar.copy(out=a_win[t][:], in_=a_ps[t][:])

        rest = z2f
        o_codes = sb.tile([P, S], U32, name="o_codes", align_bytes=64)
        o_scales = sb.tile([P, S], U8, name="o_scales", align_bytes=64)
        out_rows = out_0.rearrange("(p t) j -> p t j", t=PACK)
        out_words = out_1[0].rearrange("p n t -> p (n t)").bitcast(I32)

        def pull(c, t, pulled):
            lo, hi = CHUNKS[c]
            nc.vector.tensor_tensor(
                pulled[:, t, :], a_win[t][:].indirect(n5_t[:, lo // 16 : hi // 16]), gate[:, t, lo:hi], ALU.mult
            )

        def join(c, pulled):
            lo, hi = CHUNKS[c]
            res = sb.tile([P, PACK, hi - lo], F32, name="res%d" % c)
            nc.vector.tensor_tensor(res[:], pulled[:], rest[:, :, lo:hi], ALU.subtract)
            nc.sync.dma_start(out=out_rows[:, :, lo:hi], in_=res[:])
            return res

        def interleave(c, res):
            lo, hi = CHUNKS[c]
            rounded = sb.tile([P, PACK * (hi - lo)], BF16, name="rounded%d" % c, align_bytes=64)
            dst = rounded[:].rearrange("p (c i t) -> p c t i", i=4, t=PACK)
            src = res[:].rearrange("p t (c i) -> p c t i", i=4)
            if c == len(CHUNKS) - 1:
                nc.vector.tensor_copy(out=dst, in_=src)
            else:
                nc.scalar.activation(out=dst, in_=src, func=ACT.Copy)
            return rounded

        def quantise(c, rounded):
            lo, hi = CHUNKS[c]
            nc.vector.quantize_mx(out=o_codes[:, lo:hi].bitcast(FP8X4), scales=o_scales[:, lo:hi], in_=rounded[:])
            queue = nc.scalar if c == len(CHUNKS) - 1 else nc.sync
            queue.dma_start(out=out_words[:, lo:hi], in_=o_codes[:, lo:hi].bitcast(I32))

        pulled = [sb.tile([P, PACK, hi - lo], F32, name="pulled%d" % c) for c, (lo, hi) in enumerate(CHUNKS)]
        for t in range(PACK):
            nc.vector.scalar_tensor_tensor(
                out=rest[:, t, :], in0=gate[:, t, :], scalar=1.0, in1=a_win[t][:], op0=ALU.subtract, op1=ALU.mult
            )
            pull(0, t, pulled[0])
        pull(1, 0, pulled[1])
        r0 = interleave(0, join(0, pulled[0]))
        for t in range(1, PACK):
            pull(1, t, pulled[1])
        pull(2, 0, pulled[2])
        r1 = interleave(1, join(1, pulled[1]))
        for t in range(1, PACK):
            pull(2, t, pulled[2])
        quantise(0, r0)
        res2 = join(2, pulled[2])
        quantise(1, r1)
        quantise(2, interleave(2, res2))
        for q in range(4):
            queue = nc.sync if q % 2 == 0 else nc.scalar
            queue.dma_start(
                out=out_2[0, 4 * q : 4 * q + 4, :].bitcast(I32),
                in_=o_scales[32 * q : 32 * q + 4, :].bitcast(I32),
            )
